import numpy as np
import ml_dtypes


def mxq(x, axis, fmt="e4m3"):
    dtype, down = {"e4m3": (ml_dtypes.float8_e4m3fn, 7), "e5m2": (ml_dtypes.float8_e5m2, 14)}[fmt]
    v = np.moveaxis(np.asarray(x, np.float32).astype(ml_dtypes.bfloat16).astype(np.float64), axis, -1)
    blocks = v.reshape(v.shape[:-1] + (-1, 32))
    amax = np.abs(blocks).max(-1, keepdims=True)
    byte = np.maximum(np.where(amax > 0, np.frexp(amax)[1] - 1 + 127, 0) - down, 1)
    scale = np.exp2(byte - 127.0)
    codes = (blocks / scale).astype(np.float32).astype(dtype).astype(np.float64)
    return np.moveaxis((codes * scale).reshape(v.shape), -1, axis)


WIDE = False


def mx_kscale(k):
    if not WIDE:
        return np.ones(k)
    levels = np.array([10, -10, 5, -5, 0])
    if k % 512:
        return np.exp2(np.random.permutation(np.resize(levels, k // 32))).repeat(32)
    a = np.empty((k // 512, 16))
    for p in range(k // 512):
        a[p, :8] = np.random.permutation(np.resize(levels, 8))
        for g in range(8):
            far = levels[np.abs(levels - a[p, g]) >= 10]
            a[p, g + 8] = far[np.random.randint(len(far))]
    return np.exp2(a.ravel()).repeat(32)


def f64(x):
    return np.asarray(x).astype(np.float64)


def striped8(idx):
    return np.asarray(idx).reshape(8, -1, 16).transpose(0, 2, 1).reshape(128, -1).astype(np.uint16)


def unstriped8(offs):
    return offs.reshape(8, 16, -1).transpose(0, 2, 1).reshape(8, -1).astype(np.int64)


def pick8(x, idx, run):
    r = np.arange(len(x))
    return x[r[:, None], idx[r % (8 * run) // run]]


E2M1 = np.array([0.0, 0.5, 1.0, 1.5, 2.0, 3.0, 4.0, 6.0, -0.0, -0.5, -1.0, -1.5, -2.0, -3.0, -4.0, -6.0])


def pack_weight(w, fmt):
    k, n = w.shape
    w = f64(np.asarray(w, np.float32).astype(ml_dtypes.bfloat16)).reshape(k // 32, 32, n)
    amax = np.abs(w).max(1)
    if fmt == "e4m3":
        byte = np.frexp(amax)[1] - 1 + 127 - 7
    else:
        mant, ex = np.frexp(amax / 6.0)
        byte = np.where(mant > 0.5, ex, ex - 1) + 127
    byte = np.clip(np.where(amax > 0, byte, 1), 1, 254)
    scaled = (w * np.exp2(127.0 - byte)[:, None, :]).reshape(k, n).astype(np.float32)
    by_word = np.ascontiguousarray(scaled.reshape(k // 512, 128, 4, n).transpose(0, 1, 3, 2))
    if fmt == "e4m3":
        words = by_word.astype(ml_dtypes.float8_e4m3fn).view(np.uint8)
    else:
        c = by_word.astype(ml_dtypes.float4_e2m1fn).view(np.uint8) & 0xF
        words = (c[..., 0::2] | (c[..., 1::2] << 4)).reshape(k // 512, 128, 2 * n)
    return np.ascontiguousarray(words), np.ascontiguousarray(byte.astype(np.uint8).reshape(k // 512, 16, n))


def unpack_weight(words, scales, fmt):
    g, _, n = scales.shape
    words = np.ascontiguousarray(words).reshape(g, 128, n, -1)
    if fmt == "e4m3":
        vals = words.view(ml_dtypes.float8_e4m3fn).astype(np.float64)
    else:
        nib = np.empty((g, 128, n, 4), np.uint8)
        nib[..., 0::2] = words & 0xF
        nib[..., 1::2] = words >> 4
        vals = E2M1[nib]
    vals = vals * np.repeat(np.exp2(scales.astype(np.float64) - 127.0), 8, axis=1)[..., None]
    return vals.transpose(0, 1, 3, 2).reshape(g * 512, n)


def sigmoid(v):
    return 1.0 / (1.0 + np.exp(-v))


D, T, U, Z, I, Q = 512, 1024, 1024, 1024, 512, 128


def setup_inputs():
    n = np.random.standard_normal
    idx = np.stack([np.random.permutation(T)[:I] for _ in range(8)])
    idx2 = np.stack([np.random.permutation(U)[:I] for _ in range(8)])
    idx3 = np.stack([np.random.permutation(Z)[:I] for _ in range(8)])
    idx4 = np.stack([np.random.permutation(Z)[:I] for _ in range(8)])
    fd = mx_kscale(D)
    keysp = pack_weight(n((D, T)) / fd[:, None], "e4m3")
    notesp = pack_weight(n((D, U)) / fd[:, None], "e2m1")
    return {
        "query": (n((D, Q)) * 1.0 / np.sqrt(D) * fd[:, None]).astype(np.float32),
        "keys_words": keysp[0],
        "keys_scales": keysp[1],
        "notes_words": notesp[0],
        "notes_scales": notesp[1],
        "thr": (np.random.uniform(-0.6, 0.6, (Q, 1))).astype(np.float32),
        "slope": (np.random.uniform(1.0, 3.0, (Q, 1))).astype(np.float32),
        "offs": striped8(idx),
        "offs2": striped8(idx2),
        "offs3": striped8(idx3),
        "offs4": striped8(idx4),
    }


def reference(query, keys_words, keys_scales, notes_words, notes_scales, thr, slope, offs, offs2, offs3, offs4):
    idx = unstriped8(offs)
    idx2 = unstriped8(offs2)
    idx3 = unstriped8(offs3)
    idx4 = unstriped8(offs4)
    keysu = unpack_weight(keys_words, keys_scales, "e4m3")
    notesu = unpack_weight(notes_words, notes_scales, "e2m1")
    queryq = mxq(f64(query), 0, "e4m3")
    a = queryq.T @ keysu
    b = queryq.T @ notesu
    s1 = sigmoid(pick8(a, idx, 16) * f64(slope) + f64(thr))
    w = pick8(b, idx2, 16) * s1
    f1 = np.zeros((Q, Z))
    f1[np.arange(Q)[:, None], idx3[np.arange(Q) % 128 // 16]] = w
    v = pick8(f1, idx4, 16) - s1
    y = v * 2.0 + pick8(b, idx2, 16)
    return y

@@ -1,0 +1,140 @@
+from contextlib import ExitStack
+
+import concourse.mybir as mybir
+
+D, T, U, Z, I, Q = 512, 1024, 1024, 1024, 512, 128
+FLOPS = 2 * D * Q * (T + U)
+
+F32 = mybir.dt.float32
+BF16 = mybir.dt.bfloat16
+I32 = mybir.dt.int32
+U32 = mybir.dt.uint32
+U16 = mybir.dt.uint16
+U8 = mybir.dt.uint8
+FP8X4 = mybir.dt.float8_e4m3fn_x4
+FP4X4 = mybir.dt.float4_e2m1fn_x4
+ALU = mybir.AluOpType
+ACT = mybir.ActivationFunctionType
+
+P = 128
+PACK = 4
+B_PIECES = (512, 512)
+A_PIECES = (256, 256, 256, 128, 128)
+HALF = I // 2
+LIST_COLS = I // 16
+
+
+def load_scale_rows(queue, plane, rows):
+    for quad in range(4):
+        queue.dma_start(
+            out=plane[32 * quad : 32 * quad + 4, :].bitcast(I32),
+            in_=rows[0, 4 * quad : 4 * quad + 4, :].bitcast(I32),
+        )
+
+
+def tile_attend_openbridge_two_kernel(
+    tc, query, keys_words, keys_scales, notes_words, notes_scales, thr, slope, offs, offs2, offs3, offs4, out
+):
+    nc = tc.nc
+    with ExitStack() as ctx:
+        held = ctx.enter_context(tc.tile_pool(name="held", bufs=1))
+        psum = ctx.enter_context(tc.psum_pool(name="psum", bufs=1))
+
+        list_a = held.tile([P, LIST_COLS], U16, name="list_a")
+        list_b = held.tile([P, LIST_COLS], U16, name="list_b")
+        list_put = held.tile([P, LIST_COLS], U16, name="list_put")
+        list_f = held.tile([P, LIST_COLS], U16, name="list_f")
+
+        q_raw = held.tile([P, PACK, Q], F32, name="q_raw")
+        n_words = held.tile([P, 2 * U], U8, name="n_words", align_bytes=64)
+        n_plane = held.tile([P, U], U8, name="n_plane", align_bytes=64)
+        k_words = held.tile([P, T], U32, name="k_words", align_bytes=64)
+        k_plane = held.tile([P, T], U8, name="k_plane", align_bytes=64)
+        thr_sb = held.tile([P, 1], F32, name="thr_sb")
+        slope_sb = held.tile([P, 1], F32, name="slope_sb")
+        f1 = held.tile([P, Z], F32, name="f1")
+
+        nc.gpsimd.memset(n_plane[:].bitcast(I32), 0)
+        nc.gpsimd.memset(k_plane[:].bitcast(I32), 0)
+        warm_in = held.tile([P, 1], F32, name="warm_in")
+        warm_out = held.tile([P, 1], F32, name="warm_out")
+        nc.vector.memset(warm_in[:], 0.0)
+        nc.scalar.activation(warm_out[:], warm_in[:], ACT.Sigmoid)
+        nc.vector.memset(f1[:], 0.0)
+
+        nc.sync.dma_start(out=q_raw[:], in_=query.rearrange("(p j) q -> p j q", j=PACK))
+        load_scale_rows(nc.sync, n_plane, notes_scales)
+        nc.sync.dma_start(out=n_words[:].bitcast(I32), in_=notes_words[0].bitcast(I32))
+        nc.sync.dma_start(
+            out=k_words[:].bitcast(I32), in_=keys_words[0].rearrange("p n t -> p (n t)").bitcast(I32)
+        )
+        load_scale_rows(nc.sync, k_plane, keys_scales)
+        nc.sync.dma_start(list_b[:], offs2)
+        nc.sync.dma_start(list_a[:], offs)
+        nc.sync.dma_start(out=thr_sb[:], in_=thr)
+        nc.gpsimd.dma_start(out=slope_sb[:], in_=slope)
+        nc.sync.dma_start(list_put[:], offs3)
+        nc.sync.dma_start(list_f[:], offs4)
+
+        q_codes = held.tile([P, Q], U32, name="q_codes", align_bytes=64)
+        q_plane = held.tile([P, Q], U8, name="q_plane", align_bytes=64)
+        q_cols = [slice(h * Q // 2, (h + 1) * Q // 2) for h in range(2)]
+        q_bf = [held.tile([P, Q // 2, PACK], BF16, name="q_bf%d" % h, align_bytes=64) for h in range(2)]
+        for h in range(2):
+            nc.vector.tensor_copy(
+                out=q_bf[h][:].rearrange("p (c i) t -> p c t i", i=4),
+                in_=q_raw[:, :, q_cols[h]].rearrange("p t (c i) -> p c t i", i=4),
+            )
+        for h in range(2):
+            nc.vector.quantize_mx(
+                out=q_codes[:, q_cols[h]].bitcast(FP8X4),
+                scales=q_plane[:, q_cols[h]],
+                in_=q_bf[h][:].rearrange("p q t -> p (q t)"),
+            )
+
+        def scores(name, c0, width, words, plane):
+            bank = psum.tile([P, width], F32, name="bank_%s%d" % (name, c0))
+            nc.tensor.matmul_mx(
+                out=bank[:], lhsT=q_codes[:].bitcast(FP8X4), lhsT_scale=q_plane[:],
+                rhs=words, rhs_scale=plane[:, c0 : c0 + width], start=True, stop=True,
+            )
+            return bank
+
+        b_sb = held.tile([P, U], F32, name="b_sb")
+        a_sb = held.tile([P, T], F32, name="a_sb")
+        c0 = 0
+        for width in B_PIECES:
+            bank = scores("b", c0, width, n_words[:, 2 * c0 : 2 * (c0 + width)].bitcast(FP4X4), n_plane)
+            nc.vector.tensor_copy(out=b_sb[:, c0 : c0 + width], in_=bank[:])
+            c0 = c0 + width
+        c0 = 0
+        for width in A_PIECES:
+            bank = scores("a", c0, width, k_words[:, c0 : c0 + width].bitcast(FP8X4), k_plane)
+            nc.scalar.copy(out=a_sb[:, c0 : c0 + width], in_=bank[:])
+            c0 = c0 + width
+
+        entries = [slice(h * LIST_COLS // 2, (h + 1) * LIST_COLS // 2) for h in range(2)]
+        s1 = [held.tile([P, HALF], F32, name="s1_%d" % h) for h in range(2)]
+        bg_all = held.tile([P, I], F32, name="bg_all")
+        bg = [bg_all[:, h * HALF : (h + 1) * HALF] for h in range(2)]
+        nc.vector.tensor_copy(bg_all[:], b_sb[:].indirect(list_b[:]))
+        for h in range(2):
+            nc.scalar.activation(
+                s1[h][:], a_sb[:].indirect(list_a[:, entries[h]]), ACT.Sigmoid, bias=thr_sb[:], scale=slope_sb[:]
+            )
+
+        rest = [held.tile([P, HALF], F32, name="rest_%d" % h) for h in range(2)]
+        nc.vector.tensor_tensor(f1[:].indirect(list_put[:, entries[0]]), bg[0], s1[0][:], ALU.mult)
+        nc.vector.scalar_tensor_tensor(rest[0][:], bg[0], 0.5, s1[0][:], ALU.mult, ALU.subtract)
+        nc.vector.tensor_tensor(f1[:].indirect(list_put[:, entries[1]]), bg[1], s1[1][:], ALU.mult)
+        nc.vector.scalar_tensor_tensor(rest[1][:], s1[1][:], -2.0, bg[1], ALU.mult, ALU.add)
+
+        half_out = held.tile([P, HALF], F32, name="half_out")
+        fg = held.tile([P, HALF], F32, name="fg")
+        res = [held.tile([P, HALF], F32, name="res_%d" % h) for h in range(2)]
+        nc.vector.tensor_tensor(half_out[:], f1[:].indirect(list_f[:, entries[0]]), rest[0][:], ALU.add)
+        nc.scalar.activation(fg[:], f1[:].indirect(list_f[:, entries[1]]), ACT.Copy)
+        nc.scalar.activation(res[0][:], half_out[:], ACT.Copy, scale=2.0)
+        nc.scalar.dma_start(out=out[:, :HALF], in_=res[0][:])
+        nc.vector.scalar_tensor_tensor(res[1][:], fg[:], 2.0, rest[1][:], ALU.mult, ALU.add)
+        nc.sync.dma_start(out=out[:, HALF:], in_=res[1][:])

@@ -20,15 +20,16 @@ P = 128
 PACK = 4
 B_PIECES = (512, 512)
 A_PIECES = (256, 256, 256, 128, 128)
+K_FIRST = 4
 HALF = I // 2
 LIST_COLS = I // 16
 
 
-def load_scale_rows(queue, plane, rows):
-    for quad in range(4):
+def load_scale_rows(queue, plane, first, rows):
+    for r in range(4):
         queue.dma_start(
-            out=plane[32 * quad : 32 * quad + 4, :].bitcast(I32),
-            in_=rows[0, 4 * quad : 4 * quad + 4, :].bitcast(I32),
+            out=plane[first + r : P : 32, :].bitcast(I32),
+            in_=rows[0, r:16:4, :].bitcast(I32),
         )
 
 
@@ -54,8 +55,8 @@ def tile_attend_openbridge_two_kernel(
         slope_sb = held.tile([P, 1], F32, name="slope_sb")
         f1 = held.tile([P, Z], F32, name="f1")
 
-        nc.gpsimd.memset(n_plane[:].bitcast(I32), 0)
-        nc.gpsimd.memset(k_plane[:].bitcast(I32), 0)
+        nc.vector.memset(n_plane[:].bitcast(I32), 0)
+        nc.vector.memset(k_plane[:].bitcast(I32), 0)
         warm_in = held.tile([P, 1], F32, name="warm_in")
         warm_out = held.tile([P, 1], F32, name="warm_out")
         nc.vector.memset(warm_in[:], 0.0)
@@ -63,12 +64,12 @@ def tile_attend_openbridge_two_kernel(
         nc.vector.memset(f1[:], 0.0)
 
         nc.sync.dma_start(out=q_raw[:], in_=query.rearrange("(p j) q -> p j q", j=PACK))
-        load_scale_rows(nc.sync, n_plane, notes_scales)
+        load_scale_rows(nc.sync, n_plane, 0, notes_scales)
         nc.sync.dma_start(out=n_words[:].bitcast(I32), in_=notes_words[0].bitcast(I32))
         nc.sync.dma_start(
             out=k_words[:].bitcast(I32), in_=keys_words[0].rearrange("p n t -> p (n t)").bitcast(I32)
         )
-        load_scale_rows(nc.sync, k_plane, keys_scales)
+        load_scale_rows(nc.sync, k_plane, K_FIRST, keys_scales)
         nc.sync.dma_start(list_b[:], offs2)
         nc.sync.dma_start(list_a[:], offs)
         nc.sync.dma_start(out=thr_sb[:], in_=thr)
@@ -104,12 +105,12 @@ def tile_attend_openbridge_two_kernel(
         a_sb = held.tile([P, T], F32, name="a_sb")
         c0 = 0
         for width in B_PIECES:
-            bank = scores("b", c0, width, n_words[:, 2 * c0 : 2 * (c0 + width)].bitcast(FP4X4), n_plane)
+            bank = scores("b", c0, width, n_words[:, 2 * c0 : 2 * (c0 + width)].bitcast(FP4X4), n_plane[:])
             nc.vector.tensor_copy(out=b_sb[:, c0 : c0 + width], in_=bank[:])
             c0 = c0 + width
         c0 = 0
         for width in A_PIECES:
-            bank = scores("a", c0, width, k_words[:, c0 : c0 + width].bitcast(FP8X4), k_plane)
+            bank = scores("a", c0, width, k_words[:, c0 : c0 + width].bitcast(FP8X4), k_plane[K_FIRST:P, :])
             nc.scalar.copy(out=a_sb[:, c0 : c0 + width], in_=bank[:])
             c0 = c0 + width
 

@@ -18,15 +18,16 @@ ACT = mybir.ActivationFunctionType
 
 P = 128
 PACK = 4
-B_PIECES = (512, 512)
+B_PIECES = (512, 256, 256)
 A_PIECES = (256, 256, 256, 128, 128)
 K_FIRST = 4
+K_HALF = T // 2
 HALF = I // 2
 LIST_COLS = I // 16
 
 
-def load_scale_rows(queue, plane, first, rows):
-    for r in range(4):
+def load_scale_rows(queue, plane, first, rows, which):
+    for r in which:
         queue.dma_start(
             out=plane[first + r : P : 32, :].bitcast(I32),
             in_=rows[0, r:16:4, :].bitcast(I32),
@@ -49,7 +50,7 @@ def tile_attend_openbridge_two_kernel(
         q_raw = held.tile([P, PACK, Q], F32, name="q_raw")
         n_words = held.tile([P, 2 * U], U8, name="n_words", align_bytes=64)
         n_plane = held.tile([P, U], U8, name="n_plane", align_bytes=64)
-        k_words = held.tile([P, T], U32, name="k_words", align_bytes=64)
+        k_words = [held.tile([P, K_HALF], U32, name="k_words%d" % h, align_bytes=64) for h in range(2)]
         k_plane = held.tile([P, T], U8, name="k_plane", align_bytes=64)
         thr_sb = held.tile([P, 1], F32, name="thr_sb")
         slope_sb = held.tile([P, 1], F32, name="slope_sb")
@@ -63,13 +64,14 @@ def tile_attend_openbridge_two_kernel(
         nc.scalar.activation(warm_out[:], warm_in[:], ACT.Sigmoid)
         nc.vector.memset(f1[:], 0.0)
 
+        k_dram = keys_words[0].rearrange("p n t -> p (n t)").bitcast(I32)
         nc.sync.dma_start(out=q_raw[:], in_=query.rearrange("(p j) q -> p j q", j=PACK))
-        load_scale_rows(nc.sync, n_plane, 0, notes_scales)
+        load_scale_rows(nc.sync, n_plane, 0, notes_scales, range(4))
         nc.sync.dma_start(out=n_words[:].bitcast(I32), in_=notes_words[0].bitcast(I32))
-        nc.sync.dma_start(
-            out=k_words[:].bitcast(I32), in_=keys_words[0].rearrange("p n t -> p (n t)").bitcast(I32)
-        )
-        load_scale_rows(nc.sync, k_plane, K_FIRST, keys_scales)
+        load_scale_rows(nc.sync, k_plane, K_FIRST, keys_scales, range(1))
+        nc.sync.dma_start(out=k_words[0][:].bitcast(I32), in_=k_dram[:, :K_HALF])
+        load_scale_rows(nc.sync, k_plane, K_FIRST, keys_scales, range(1, 4))
+        nc.sync.dma_start(out=k_words[1][:].bitcast(I32), in_=k_dram[:, K_HALF:])
         nc.sync.dma_start(list_b[:], offs2)
         nc.sync.dma_start(list_a[:], offs)
         nc.sync.dma_start(out=thr_sb[:], in_=thr)
@@ -106,11 +108,14 @@ def tile_attend_openbridge_two_kernel(
         c0 = 0
         for width in B_PIECES:
             bank = scores("b", c0, width, n_words[:, 2 * c0 : 2 * (c0 + width)].bitcast(FP4X4), n_plane[:])
-            nc.vector.tensor_copy(out=b_sb[:, c0 : c0 + width], in_=bank[:])
+            if c0 == 0:
+                nc.scalar.copy(out=b_sb[:, c0 : c0 + width], in_=bank[:])
+            else:
+                nc.vector.tensor_copy(out=b_sb[:, c0 : c0 + width], in_=bank[:])
             c0 = c0 + width
         c0 = 0
         for width in A_PIECES:
-            bank = scores("a", c0, width, k_words[:, c0 : c0 + width].bitcast(FP8X4), k_plane[K_FIRST:P, :])
+            bank = scores("a", c0, width, k_words[c0 // K_HALF][:, c0 % K_HALF : c0 % K_HALF + width].bitcast(FP8X4), k_plane[K_FIRST:P, :])
             nc.scalar.copy(out=a_sb[:, c0 : c0 + width], in_=bank[:])
             c0 = c0 + width
 

from contextlib import ExitStack

import concourse.mybir as mybir

D, T, U, Z, I, Q = 512, 1024, 1024, 1024, 512, 128
FLOPS = 2 * D * Q * (T + U)

F32 = mybir.dt.float32
BF16 = mybir.dt.bfloat16
I32 = mybir.dt.int32
U32 = mybir.dt.uint32
U16 = mybir.dt.uint16
U8 = mybir.dt.uint8
FP8X4 = mybir.dt.float8_e4m3fn_x4
FP4X4 = mybir.dt.float4_e2m1fn_x4
ALU = mybir.AluOpType
ACT = mybir.ActivationFunctionType

P = 128
PACK = 4
B_PIECES = (512, 256, 256)
A_PIECES = (256, 256, 256, 128, 128)
K_FIRST = 4
K_HALF = T // 2
HALF = I // 2
LIST_COLS = I // 16


def load_scale_rows(queue, plane, first, rows, which):
    for r in which:
        queue.dma_start(
            out=plane[first + r : P : 32, :].bitcast(I32),
            in_=rows[0, r:16:4, :].bitcast(I32),
        )


def tile_attend_openbridge_two_kernel(
    tc, query, keys_words, keys_scales, notes_words, notes_scales, thr, slope, offs, offs2, offs3, offs4, out
):
    nc = tc.nc
    with ExitStack() as ctx:
        held = ctx.enter_context(tc.tile_pool(name="held", bufs=1))
        psum = ctx.enter_context(tc.psum_pool(name="psum", bufs=1))

        list_a = held.tile([P, LIST_COLS], U16, name="list_a")
        list_b = held.tile([P, LIST_COLS], U16, name="list_b")
        list_put = held.tile([P, LIST_COLS], U16, name="list_put")
        list_f = held.tile([P, LIST_COLS], U16, name="list_f")

        q_raw = held.tile([P, PACK, Q], F32, name="q_raw")
        n_words = held.tile([P, 2 * U], U8, name="n_words", align_bytes=64)
        n_plane = held.tile([P, U], U8, name="n_plane", align_bytes=64)
        k_words = [held.tile([P, K_HALF], U32, name="k_words%d" % h, align_bytes=64) for h in range(2)]
        k_plane = held.tile([P, T], U8, name="k_plane", align_bytes=64)
        thr_sb = held.tile([P, 1], F32, name="thr_sb")
        slope_sb = held.tile([P, 1], F32, name="slope_sb")
        f1 = held.tile([P, Z], F32, name="f1")

        nc.vector.memset(n_plane[:].bitcast(I32), 0)
        nc.vector.memset(k_plane[:].bitcast(I32), 0)
        warm_in = held.tile([P, 1], F32, name="warm_in")
        warm_out = held.tile([P, 1], F32, name="warm_out")
        nc.vector.memset(warm_in[:], 0.0)
        nc.scalar.activation(warm_out[:], warm_in[:], ACT.Sigmoid)
        nc.vector.memset(f1[:], 0.0)

        k_dram = keys_words[0].rearrange("p n t -> p (n t)").bitcast(I32)
        nc.sync.dma_start(out=q_raw[:], in_=query.rearrange("(p j) q -> p j q", j=PACK))
        load_scale_rows(nc.sync, n_plane, 0, notes_scales, range(4))
        nc.sync.dma_start(out=n_words[:].bitcast(I32), in_=notes_words[0].bitcast(I32))
        load_scale_rows(nc.sync, k_plane, K_FIRST, keys_scales, range(1))
        nc.sync.dma_start(out=k_words[0][:].bitcast(I32), in_=k_dram[:, :K_HALF])
        load_scale_rows(nc.sync, k_plane, K_FIRST, keys_scales, range(1, 4))
        nc.sync.dma_start(out=k_words[1][:].bitcast(I32), in_=k_dram[:, K_HALF:])
        nc.sync.dma_start(list_b[:], offs2)
        nc.sync.dma_start(list_a[:], offs)
        nc.sync.dma_start(out=thr_sb[:], in_=thr)
        nc.gpsimd.dma_start(out=slope_sb[:], in_=slope)
        nc.sync.dma_start(list_put[:], offs3)
        nc.sync.dma_start(list_f[:], offs4)

        q_codes = held.tile([P, Q], U32, name="q_codes", align_bytes=64)
        q_plane = held.tile([P, Q], U8, name="q_plane", align_bytes=64)
        q_cols = [slice(h * Q // 2, (h + 1) * Q // 2) for h in range(2)]
        q_bf = [held.tile([P, Q // 2, PACK], BF16, name="q_bf%d" % h, align_bytes=64) for h in range(2)]
        for h in range(2):
            nc.vector.tensor_copy(
                out=q_bf[h][:].rearrange("p (c i) t -> p c t i", i=4),
                in_=q_raw[:, :, q_cols[h]].rearrange("p t (c i) -> p c t i", i=4),
            )
        for h in range(2):
            nc.vector.quantize_mx(
                out=q_codes[:, q_cols[h]].bitcast(FP8X4),
                scales=q_plane[:, q_cols[h]],
                in_=q_bf[h][:].rearrange("p q t -> p (q t)"),
            )

        def scores(name, c0, width, words, plane):
            bank = psum.tile([P, width], F32, name="bank_%s%d" % (name, c0))
            nc.tensor.matmul_mx(
                out=bank[:], lhsT=q_codes[:].bitcast(FP8X4), lhsT_scale=q_plane[:],
                rhs=words, rhs_scale=plane[:, c0 : c0 + width], start=True, stop=True,
            )
            return bank

        b_sb = held.tile([P, U], F32, name="b_sb")
        a_sb = held.tile([P, T], F32, name="a_sb")
        c0 = 0
        for width in B_PIECES:
            bank = scores("b", c0, width, n_words[:, 2 * c0 : 2 * (c0 + width)].bitcast(FP4X4), n_plane[:])
            if c0 == 0:
                nc.scalar.copy(out=b_sb[:, c0 : c0 + width], in_=bank[:])
            else:
                nc.vector.tensor_copy(out=b_sb[:, c0 : c0 + width], in_=bank[:])
            c0 = c0 + width
        c0 = 0
        for width in A_PIECES:
            bank = scores("a", c0, width, k_words[c0 // K_HALF][:, c0 % K_HALF : c0 % K_HALF + width].bitcast(FP8X4), k_plane[K_FIRST:P, :])
            nc.scalar.copy(out=a_sb[:, c0 : c0 + width], in_=bank[:])
            c0 = c0 + width

        entries = [slice(h * LIST_COLS // 2, (h + 1) * LIST_COLS // 2) for h in range(2)]
        s1 = [held.tile([P, HALF], F32, name="s1_%d" % h) for h in range(2)]
        bg_all = held.tile([P, I], F32, name="bg_all")
        bg = [bg_all[:, h * HALF : (h + 1) * HALF] for h in range(2)]
        nc.vector.tensor_copy(bg_all[:], b_sb[:].indirect(list_b[:]))
        for h in range(2):
            nc.scalar.activation(
                s1[h][:], a_sb[:].indirect(list_a[:, entries[h]]), ACT.Sigmoid, bias=thr_sb[:], scale=slope_sb[:]
            )

        rest = [held.tile([P, HALF], F32, name="rest_%d" % h) for h in range(2)]
        nc.vector.tensor_tensor(f1[:].indirect(list_put[:, entries[0]]), bg[0], s1[0][:], ALU.mult)
        nc.vector.scalar_tensor_tensor(rest[0][:], bg[0], 0.5, s1[0][:], ALU.mult, ALU.subtract)
        nc.vector.tensor_tensor(f1[:].indirect(list_put[:, entries[1]]), bg[1], s1[1][:], ALU.mult)
        nc.vector.scalar_tensor_tensor(rest[1][:], s1[1][:], -2.0, bg[1], ALU.mult, ALU.add)

        half_out = held.tile([P, HALF], F32, name="half_out")
        fg = held.tile([P, HALF], F32, name="fg")
        res = [held.tile([P, HALF], F32, name="res_%d" % h) for h in range(2)]
        nc.vector.tensor_tensor(half_out[:], f1[:].indirect(list_f[:, entries[0]]), rest[0][:], ALU.add)
        nc.scalar.activation(fg[:], f1[:].indirect(list_f[:, entries[1]]), ACT.Copy)
        nc.scalar.activation(res[0][:], half_out[:], ACT.Copy, scale=2.0)
        nc.scalar.dma_start(out=out[:, :HALF], in_=res[0][:])
        nc.vector.scalar_tensor_tensor(res[1][:], fg[:], 2.0, rest[1][:], ALU.mult, ALU.add)
        nc.sync.dma_start(out=out[:, HALF:], in_=res[1][:])
